import numpy as np
import ml_dtypes


def mxq(x, axis, fmt="e4m3"):
    dtype, down = {"e4m3": (ml_dtypes.float8_e4m3fn, 7), "e5m2": (ml_dtypes.float8_e5m2, 14)}[fmt]
    v = np.moveaxis(np.asarray(x, np.float32).astype(ml_dtypes.bfloat16).astype(np.float64), axis, -1)
    blocks = v.reshape(v.shape[:-1] + (-1, 32))
    amax = np.abs(blocks).max(-1, keepdims=True)
    byte = np.maximum(np.where(amax > 0, np.frexp(amax)[1] - 1 + 127, 0) - down, 1)
    scale = np.exp2(byte - 127.0)
    codes = (blocks / scale).astype(np.float32).astype(dtype).astype(np.float64)
    return np.moveaxis((codes * scale).reshape(v.shape), -1, axis)


WIDE = False


def mx_kscale(k):
    if not WIDE:
        return np.ones(k)
    levels = np.array([10, -10, 5, -5, 0])
    if k % 512:
        return np.exp2(np.random.permutation(np.resize(levels, k // 32))).repeat(32)
    a = np.empty((k // 512, 16))
    for p in range(k // 512):
        a[p, :8] = np.random.permutation(np.resize(levels, 8))
        for g in range(8):
            far = levels[np.abs(levels - a[p, g]) >= 10]
            a[p, g + 8] = far[np.random.randint(len(far))]
    return np.exp2(a.ravel()).repeat(32)


def f64(x):
    return np.asarray(x).astype(np.float64)


def striped(idx):
    return np.tile(idx.reshape(-1, 16).T, (8, 1)).astype(np.uint16)


def unstriped(offs):
    return offs[:16].T.reshape(-1).astype(np.int64)


def pack_weight(w):
    k, n = w.shape
    w = f64(np.asarray(w, np.float32).astype(ml_dtypes.bfloat16)).reshape(k // 32, 32, n)
    amax = np.abs(w).max(1)
    byte = np.clip(np.where(amax > 0, np.frexp(amax)[1] - 1 + 127 - 7, 1), 1, 254)
    scaled = (w * np.exp2(127.0 - byte)[:, None, :]).reshape(k, n).astype(np.float32)
    words = np.ascontiguousarray(scaled.reshape(k // 512, 128, 4, n).transpose(0, 1, 3, 2)).astype(ml_dtypes.float8_e4m3fn).view(np.uint8)
    return words, np.ascontiguousarray(byte.astype(np.uint8).reshape(k // 512, 16, n))


def unpack_weight(words, scales):
    g, p, n, _ = words.shape
    vals = np.ascontiguousarray(words).view(ml_dtypes.float8_e4m3fn).astype(np.float64) * np.repeat(np.exp2(scales.astype(np.float64) - 127.0), 8, axis=1)[..., None]
    return vals.transpose(0, 1, 3, 2).reshape(g * 512, n)


K, T, S, H, N = 1024, 2048, 512, 512, 128


def setup_inputs():
    n = np.random.standard_normal
    s = mx_kscale(K)[:, None]
    u = mx_kscale(H)
    packed_w1 = pack_weight(n((K, N)) / np.sqrt(2 * K) / s)
    packed_w3 = pack_weight(n((H, N)) / np.sqrt(2 * H) / u[:, None])
    return {
        "xT": (n((K, T)) * s).astype(np.float32),
        "w1_words": packed_w1[0],
        "w1_scales": packed_w1[1],
        "w2": (n((K, H)) / np.sqrt(K) / s * u).astype(np.float32),
        "w3_words": packed_w3[0],
        "w3_scales": packed_w3[1],
        "offs": striped(np.random.permutation(T)[:S]),
    }


def reference(xT, w1_words, w1_scales, w2, w3_words, w3_scales, offs):
    xq = mxq(f64(xT)[:, unstriped(offs)], 0, "e4m3")
    h = mxq(f64(w2), 0, "e4m3").T @ xq
    return unpack_weight(w1_words, w1_scales).T @ xq + unpack_weight(w3_words, w3_scales).T @ mxq(h, 0, "e4m3")

@@ -1,0 +1,123 @@
+from contextlib import ExitStack
+
+import concourse.mybir as mybir
+
+K, T, S, H, N = 1024, 2048, 512, 512, 128
+FLOPS = 2 * S * (K * H + K * N + H * N)
+
+F32 = mybir.dt.float32
+BF16 = mybir.dt.bfloat16
+I32 = mybir.dt.int32
+U32 = mybir.dt.uint32
+U16 = mybir.dt.uint16
+U8 = mybir.dt.uint8
+FP8X4 = mybir.dt.float8_e4m3fn_x4
+
+P = 128
+PACK = 4
+KP = P * PACK
+CH = 128
+NCH = S // CH
+LAST_SCALAR_M = 20
+
+
+def tile_picked_lora_none_e_kernel(tc, xT, w1_words, w1_scales, w2, w3_words, w3_scales, offs, out):
+    nc = tc.nc
+    with ExitStack() as ctx:
+        keep = ctx.enter_context(tc.tile_pool(name="keep", bufs=1))
+        psum = ctx.enter_context(tc.psum_pool(name="psum", bufs=1))
+
+        offsets = keep.tile([P, S // 16], U16, name="offsets")
+        nc.sync.dma_start(offsets[:], offs)
+
+        s1 = keep.tile([P, 2, N], U8, name="s1", align_bytes=64)
+        s3 = keep.tile([P, N], U8, name="s3", align_bytes=64)
+        nc.gpsimd.memset(s1[:], 0)
+        nc.gpsimd.memset(s3[:], 0)
+        for r in range(4):
+            nc.gpsimd.dma_start(s1[r:P:32, :, :].bitcast(I32), w1_scales[:, r:16:4, :].rearrange("z q c -> q z c").bitcast(I32))
+        for r in range(4):
+            nc.gpsimd.dma_start(s3[r:P:32, :].bitcast(I32), w3_scales[0, r:16:4, :].bitcast(I32))
+
+        w2g = [keep.tile([P, PACK, P, PACK], BF16, name=f"w2g{z}", align_bytes=64) for z in range(2)]
+        w2q = [keep.tile([P, H], U32, name=f"w2q{z}", align_bytes=64) for z in range(2)]
+        w2s = [keep.tile([P, H], U8, name=f"w2s{z}", align_bytes=64) for z in range(2)]
+        xg = [keep.tile([P, S, PACK], BF16, name=f"xg{z}", align_bytes=64) for z in range(2)]
+        xq = [keep.tile([P, S], U32, name=f"xq{z}", align_bytes=64) for z in range(2)]
+        xs = [keep.tile([P, S], U8, name=f"xs{z}", align_bytes=64) for z in range(2)]
+        hbank = [psum.tile([P, PACK, CH], F32, name=f"hbank{c}") for c in range(NCH)]
+        obank = [psum.tile([P, CH], F32, name=f"obank{c}") for c in range(NCH)]
+
+        def load_w2(z, c0, c1):
+            raw = keep.tile([P, PACK, c1 - c0], F32, name=f"w2raw{z}_{c0}")
+            nc.sync.dma_start(raw[:], w2[z * KP:(z + 1) * KP, c0:c1].rearrange("(p j) c -> p j c", j=PACK))
+            return raw
+
+        def deal_w2(copy, z, raw, c0, m0, m1):
+            src = raw[:, :, PACK * m0 - c0:PACK * m1 - c0].rearrange("p j (m t) -> p m j t", t=PACK)
+            copy(w2g[z][:, :, m0:m1, :].rearrange("p t m j -> p m j t"), src)
+
+        def plane(z, j):
+            win = keep.tile([P, T], F32, name=f"x{z}_{j}")
+            nc.sync.dma_start(win[:], xT[z * KP + j:(z + 1) * KP:PACK, :])
+            nc.vector.tensor_copy(xg[z][:, :, j], win[:].indirect(offsets[:]))
+
+        def quant_x(z):
+            nc.vector.quantize_mx(xq[z][:].bitcast(FP8X4), xs[z][:], xg[z][:].rearrange("p s j -> p (s j)"))
+
+        def mm(dst, lq, ls, rq, rs, start, stop):
+            nc.tensor.matmul_mx(dst, lq.bitcast(FP8X4), ls, rq.bitcast(FP8X4), rs, start=start, stop=stop)
+
+        def h_pass(z, c, t):
+            cols = slice(c * CH, (c + 1) * CH)
+            ws = slice(t * P, (t + 1) * P)
+            mm(hbank[c][:, t, :], w2q[z][:, ws], w2s[z][:, ws], xq[z][:, cols], xs[z][:, cols],
+               z == 0 and t == 0, z == 1 and t == PACK - 1)
+
+        def w1_pass(z, c):
+            cols = slice(c * CH, (c + 1) * CH)
+            mm(obank[c][:], w1q[:, z, :], s1[:, z, :], xq[z][:, cols], xs[z][:, cols], z == 0, False)
+
+        raw0 = load_w2(0, 0, H)
+        deal_w2(nc.scalar.copy, 0, raw0, 0, 0, P)
+        nc.vector.quantize_mx(w2q[0][:].bitcast(FP8X4), w2s[0][:], w2g[0][:].rearrange("p t m j -> p (t m j)"))
+        for j in range(3):
+            plane(1, j)
+        w1q = keep.tile([P, 2, N], U32, name="w1q", align_bytes=64)
+        nc.sync.dma_start(w1q[:].bitcast(I32), w1_words.rearrange("z p n t -> p z (n t)").bitcast(I32))
+        w3q = keep.tile([P, N], U32, name="w3q", align_bytes=64)
+        nc.sync.dma_start(w3q[:].bitcast(I32), w3_words[0].rearrange("p n t -> p (n t)").bitcast(I32))
+        for j in range(4):
+            plane(0, j)
+        quant_x(0)
+        for c in range(NCH):
+            w1_pass(0, c)
+        for c in range(NCH):
+            for t in range(PACK):
+                h_pass(0, c, t)
+        plane(1, 3)
+        quant_x(1)
+        for c in range(NCH):
+            w1_pass(1, c)
+        raw1a = load_w2(1, 0, H // 2)
+        raw1b = load_w2(1, H // 2, H)
+        deal_w2(nc.scalar.copy, 1, raw1a, 0, 0, P // 2)
+        deal_w2(nc.scalar.copy, 1, raw1b, H // 2, P // 2, P // 2 + LAST_SCALAR_M)
+        deal_w2(nc.vector.tensor_copy, 1, raw1b, H // 2, P // 2 + LAST_SCALAR_M, P)
+        for t in range(PACK):
+            ws = slice(t * P, (t + 1) * P)
+            nc.vector.quantize_mx(w2q[1][:, ws].bitcast(FP8X4), w2s[1][:, ws], w2g[1][:, t, :, :].rearrange("p m j -> p (m j)"))
+        for c in range(NCH):
+            for t in range(PACK):
+                h_pass(1, c, t)
+        for c in range(NCH):
+            copy = nc.scalar.copy if c % 2 == 0 else nc.vector.tensor_copy
+            hg = keep.tile([P, CH, PACK], BF16, name=f"hg{c}", align_bytes=64)
+            copy(hg[:], hbank[c][:].rearrange("p t n -> p n t"))
+            hq = keep.tile([P, CH], U32, name=f"hq{c}", align_bytes=64)
+            hs = keep.tile([P, CH], U8, name=f"hs{c}", align_bytes=64)
+            nc.vector.quantize_mx(hq[:].bitcast(FP8X4), hs[:], hg[:].rearrange("p n t -> p (n t)"))
+            mm(obank[c][:], w3q[:], s3[:], hq[:], hs[:], False, True)
+            res = keep.tile([P, CH], F32, name=f"res{c}")
+            nc.scalar.copy(res[:], obank[c][:])
+            nc.sync.dma_start(out[:, c * CH:(c + 1) * CH], res[:])

@@ -18,7 +18,6 @@ PACK = 4
 KP = P * PACK
 CH = 128
 NCH = S // CH
-LAST_SCALAR_M = 20
 
 
 def tile_picked_lora_none_e_kernel(tc, xT, w1_words, w1_scales, w2, w3_words, w3_scales, offs, out):
@@ -28,17 +27,11 @@ def tile_picked_lora_none_e_kernel(tc, xT, w1_words, w1_scales, w2, w3_words, w3
         psum = ctx.enter_context(tc.psum_pool(name="psum", bufs=1))
 
         offsets = keep.tile([P, S // 16], U16, name="offsets")
-        nc.sync.dma_start(offsets[:], offs)
 
         s1 = keep.tile([P, 2, N], U8, name="s1", align_bytes=64)
         s3 = keep.tile([P, N], U8, name="s3", align_bytes=64)
-        nc.gpsimd.memset(s1[:], 0)
-        nc.gpsimd.memset(s3[:], 0)
-        for r in range(4):
-            nc.gpsimd.dma_start(s1[r:P:32, :, :].bitcast(I32), w1_scales[:, r:16:4, :].rearrange("z q c -> q z c").bitcast(I32))
-        for r in range(4):
-            nc.gpsimd.dma_start(s3[r:P:32, :].bitcast(I32), w3_scales[0, r:16:4, :].bitcast(I32))
-
+        nc.vector.memset(s1[:], 0)
+        nc.vector.memset(s3[:], 0)
         w2g = [keep.tile([P, PACK, P, PACK], BF16, name=f"w2g{z}", align_bytes=64) for z in range(2)]
         w2q = [keep.tile([P, H], U32, name=f"w2q{z}", align_bytes=64) for z in range(2)]
         w2s = [keep.tile([P, H], U8, name=f"w2s{z}", align_bytes=64) for z in range(2)]
@@ -53,14 +46,24 @@ def tile_picked_lora_none_e_kernel(tc, xT, w1_words, w1_scales, w2, w3_words, w3
             nc.sync.dma_start(raw[:], w2[z * KP:(z + 1) * KP, c0:c1].rearrange("(p j) c -> p j c", j=PACK))
             return raw
 
-        def deal_w2(copy, z, raw, c0, m0, m1):
-            src = raw[:, :, PACK * m0 - c0:PACK * m1 - c0].rearrange("p j (m t) -> p m j t", t=PACK)
-            copy(w2g[z][:, :, m0:m1, :].rearrange("p t m j -> p m j t"), src)
+        def deal_w2(copy, z, raw, m0, m1, t0, t1):
+            src = raw[:].rearrange("p j (m t) -> p m t j", t=PACK)[:, :, t0:t1, :]
+            copy(w2g[z][:, t0:t1, m0:m1, :].rearrange("p t m j -> p m t j"), src)
 
-        def plane(z, j):
+        def load_x(z, j):
             win = keep.tile([P, T], F32, name=f"x{z}_{j}")
             nc.sync.dma_start(win[:], xT[z * KP + j:(z + 1) * KP:PACK, :])
+            return win
+
+        def gather(z, j, win):
             nc.vector.tensor_copy(xg[z][:, :, j], win[:].indirect(offsets[:]))
+
+        def plane(z, j):
+            gather(z, j, load_x(z, j))
+
+        def load_scales(r):
+            nc.sync.dma_start(s1[r:P:32, :, :].bitcast(I32), w1_scales[:, r:16:4, :].rearrange("z q c -> q z c").bitcast(I32))
+            nc.sync.dma_start(s3[r:P:32, :].bitcast(I32), w3_scales[0, r:16:4, :].bitcast(I32))
 
         def quant_x(z):
             nc.vector.quantize_mx(xq[z][:].bitcast(FP8X4), xs[z][:], xg[z][:].rearrange("p s j -> p (s j)"))
@@ -78,40 +81,46 @@ def tile_picked_lora_none_e_kernel(tc, xT, w1_words, w1_scales, w2, w3_words, w3
             cols = slice(c * CH, (c + 1) * CH)
             mm(obank[c][:], w1q[:, z, :], s1[:, z, :], xq[z][:, cols], xs[z][:, cols], z == 0, False)
 
-        raw0 = load_w2(0, 0, H)
-        deal_w2(nc.scalar.copy, 0, raw0, 0, 0, P)
-        nc.vector.quantize_mx(w2q[0][:].bitcast(FP8X4), w2s[0][:], w2g[0][:].rearrange("p t m j -> p (t m j)"))
-        for j in range(3):
-            plane(1, j)
-        w1q = keep.tile([P, 2, N], U32, name="w1q", align_bytes=64)
-        nc.sync.dma_start(w1q[:].bitcast(I32), w1_words.rearrange("z p n t -> p z (n t)").bitcast(I32))
-        w3q = keep.tile([P, N], U32, name="w3q", align_bytes=64)
-        nc.sync.dma_start(w3q[:].bitcast(I32), w3_words[0].rearrange("p n t -> p (n t)").bitcast(I32))
-        for j in range(4):
+        first = load_x(0, 0)
+        nc.sync.dma_start(offsets[:], offs)
+        gather(0, 0, first)
+        for j in range(1, 4):
             plane(0, j)
+            load_scales(j - 1)
         quant_x(0)
-        for c in range(NCH):
-            w1_pass(0, c)
+        plane(1, 0)
+        load_scales(3)
+        for j in range(1, 3):
+            plane(1, j)
+        raw0 = load_w2(0, 0, H)
+        deal_w2(nc.scalar.copy, 0, raw0, 0, P, 0, 1)
+        deal_w2(nc.vector.tensor_copy, 0, raw0, 0, P, 1, PACK)
+        nc.vector.quantize_mx(w2q[0][:].bitcast(FP8X4), w2s[0][:], w2g[0][:].rearrange("p t m j -> p (t m j)"))
         for c in range(NCH):
             for t in range(PACK):
                 h_pass(0, c, t)
         plane(1, 3)
         quant_x(1)
-        for c in range(NCH):
-            w1_pass(1, c)
         raw1a = load_w2(1, 0, H // 2)
         raw1b = load_w2(1, H // 2, H)
-        deal_w2(nc.scalar.copy, 1, raw1a, 0, 0, P // 2)
-        deal_w2(nc.scalar.copy, 1, raw1b, H // 2, P // 2, P // 2 + LAST_SCALAR_M)
-        deal_w2(nc.vector.tensor_copy, 1, raw1b, H // 2, P // 2 + LAST_SCALAR_M, P)
-        for t in range(PACK):
-            ws = slice(t * P, (t + 1) * P)
-            nc.vector.quantize_mx(w2q[1][:, ws].bitcast(FP8X4), w2s[1][:, ws], w2g[1][:, t, :, :].rearrange("p m j -> p (m j)"))
+        w1q = keep.tile([P, 2, N], U32, name="w1q", align_bytes=64)
+        nc.sync.dma_start(w1q[:].bitcast(I32), w1_words.rearrange("z p n t -> p z (n t)").bitcast(I32))
+        w3q = keep.tile([P, N], U32, name="w3q", align_bytes=64)
+        nc.sync.dma_start(w3q[:].bitcast(I32), w3_words[0].rearrange("p n t -> p (n t)").bitcast(I32))
+        deal_w2(nc.scalar.copy, 1, raw1a, 0, P // 2, 0, PACK)
+        deal_w2(nc.scalar.copy, 1, raw1b, P // 2, P, 3, PACK)
+        deal_w2(nc.vector.tensor_copy, 1, raw1b, P // 2, P, 0, 3)
+        for t in range(0, PACK, 2):
+            ws = slice(t * P, (t + 2) * P)
+            nc.vector.quantize_mx(w2q[1][:, ws].bitcast(FP8X4), w2s[1][:, ws], w2g[1][:, t:t + 2, :, :].rearrange("p t m j -> p (t m j)"))
         for c in range(NCH):
             for t in range(PACK):
                 h_pass(1, c, t)
         for c in range(NCH):
-            copy = nc.scalar.copy if c % 2 == 0 else nc.vector.tensor_copy
+            w1_pass(0, c)
+            w1_pass(1, c)
+        for c in range(NCH):
+            copy = nc.scalar.copy if c % 2 == 1 else nc.vector.tensor_copy
             hg = keep.tile([P, CH, PACK], BF16, name=f"hg{c}", align_bytes=64)
             copy(hg[:], hbank[c][:].rearrange("p t n -> p n t"))
             hq = keep.tile([P, CH], U32, name=f"hq{c}", align_bytes=64)

@@ -16,6 +16,9 @@ FP8X4 = mybir.dt.float8_e4m3fn_x4
 P = 128
 PACK = 4
 KP = P * PACK
+PASSES = K // KP
+QUADRANT = 32
+BLOCKS = KP // 32
 CH = 128
 NCH = S // CH
 
@@ -28,105 +31,121 @@ def tile_picked_lora_none_e_kernel(tc, xT, w1_words, w1_scales, w2, w3_words, w3
 
         offsets = keep.tile([P, S // 16], U16, name="offsets")
 
-        s1 = keep.tile([P, 2, N], U8, name="s1", align_bytes=64)
+        s1 = keep.tile([P, PASSES, N], U8, name="s1", align_bytes=64)
         s3 = keep.tile([P, N], U8, name="s3", align_bytes=64)
         nc.vector.memset(s1[:], 0)
         nc.vector.memset(s3[:], 0)
-        w2g = [keep.tile([P, PACK, P, PACK], BF16, name=f"w2g{z}", align_bytes=64) for z in range(2)]
-        w2q = [keep.tile([P, H], U32, name=f"w2q{z}", align_bytes=64) for z in range(2)]
-        w2s = [keep.tile([P, H], U8, name=f"w2s{z}", align_bytes=64) for z in range(2)]
-        xg = [keep.tile([P, S, PACK], BF16, name=f"xg{z}", align_bytes=64) for z in range(2)]
-        xq = [keep.tile([P, S], U32, name=f"xq{z}", align_bytes=64) for z in range(2)]
-        xs = [keep.tile([P, S], U8, name=f"xs{z}", align_bytes=64) for z in range(2)]
+
+        w2g = [keep.tile([P, PACK, P, PACK], BF16, name=f"w2g{z}", align_bytes=64) for z in range(PASSES)]
+        w2q = [keep.tile([P, H], U32, name=f"w2q{z}", align_bytes=64) for z in range(PASSES)]
+        w2s = [keep.tile([P, H], U8, name=f"w2s{z}", align_bytes=64) for z in range(PASSES)]
+        xg = [keep.tile([P, S, PACK], BF16, name=f"xg{z}", align_bytes=64) for z in range(PASSES)]
+        xq = [keep.tile([P, S], U32, name=f"xq{z}", align_bytes=64) for z in range(PASSES)]
+        xs = [keep.tile([P, S], U8, name=f"xs{z}", align_bytes=64) for z in range(PASSES)]
+
         hbank = [psum.tile([P, PACK, CH], F32, name=f"hbank{c}") for c in range(NCH)]
         obank = [psum.tile([P, CH], F32, name=f"obank{c}") for c in range(NCH)]
 
-        def load_w2(z, c0, c1):
-            raw = keep.tile([P, PACK, c1 - c0], F32, name=f"w2raw{z}_{c0}")
-            nc.sync.dma_start(raw[:], w2[z * KP:(z + 1) * KP, c0:c1].rearrange("(p j) c -> p j c", j=PACK))
+        def load_w2(z, col0, col1):
+            raw = keep.tile([P, PACK, col1 - col0], F32, name=f"w2raw{z}_{col0}")
+            nc.sync.dma_start(raw[:], w2[z * KP:(z + 1) * KP, col0:col1].rearrange("(p j) c -> p j c", j=PACK))
             return raw
 
         def deal_w2(copy, z, raw, m0, m1, t0, t1):
             src = raw[:].rearrange("p j (m t) -> p m t j", t=PACK)[:, :, t0:t1, :]
             copy(w2g[z][:, t0:t1, m0:m1, :].rearrange("p t m j -> p m t j"), src)
 
+        def quantise_w2(z, t0, t1):
+            cols = slice(t0 * P, t1 * P)
+            values = w2g[z][:, t0:t1, :, :].rearrange("p t m j -> p (t m j)")
+            nc.vector.quantize_mx(w2q[z][:, cols].bitcast(FP8X4), w2s[z][:, cols], values)
+
         def load_x(z, j):
             win = keep.tile([P, T], F32, name=f"x{z}_{j}")
             nc.sync.dma_start(win[:], xT[z * KP + j:(z + 1) * KP:PACK, :])
             return win
 
-        def gather(z, j, win):
+        def gather_x(z, j, win):
             nc.vector.tensor_copy(xg[z][:, :, j], win[:].indirect(offsets[:]))
 
-        def plane(z, j):
-            gather(z, j, load_x(z, j))
-
-        def load_scales(r):
-            nc.sync.dma_start(s1[r:P:32, :, :].bitcast(I32), w1_scales[:, r:16:4, :].rearrange("z q c -> q z c").bitcast(I32))
-            nc.sync.dma_start(s3[r:P:32, :].bitcast(I32), w3_scales[0, r:16:4, :].bitcast(I32))
-
-        def quant_x(z):
+        def quantise_x(z):
             nc.vector.quantize_mx(xq[z][:].bitcast(FP8X4), xs[z][:], xg[z][:].rearrange("p s j -> p (s j)"))
 
-        def mm(dst, lq, ls, rq, rs, start, stop):
-            nc.tensor.matmul_mx(dst, lq.bitcast(FP8X4), ls, rq.bitcast(FP8X4), rs, start=start, stop=stop)
+        def load_w1_scales(r):
+            rows = w1_scales[:, r:BLOCKS:PACK, :].rearrange("z q c -> q z c")
+            nc.sync.dma_start(s1[r:P:QUADRANT, :, :].bitcast(I32), rows.bitcast(I32))
 
-        def h_pass(z, c, t):
-            cols = slice(c * CH, (c + 1) * CH)
-            ws = slice(t * P, (t + 1) * P)
-            mm(hbank[c][:, t, :], w2q[z][:, ws], w2s[z][:, ws], xq[z][:, cols], xs[z][:, cols],
-               z == 0 and t == 0, z == 1 and t == PACK - 1)
+        def load_w3_scales(r):
+            nc.sync.dma_start(s3[r:P:QUADRANT, :].bitcast(I32), w3_scales[0, r:BLOCKS:PACK, :].bitcast(I32))
 
-        def w1_pass(z, c):
-            cols = slice(c * CH, (c + 1) * CH)
-            mm(obank[c][:], w1q[:, z, :], s1[:, z, :], xq[z][:, cols], xs[z][:, cols], z == 0, False)
+        def mm(dst, lhs_words, lhs_scales, rhs_words, rhs_scales, start, stop):
+            nc.tensor.matmul_mx(dst, lhs_words.bitcast(FP8X4), lhs_scales, rhs_words.bitcast(FP8X4), rhs_scales,
+                                start=start, stop=stop)
+
+        def h_pass(z):
+            for c in range(NCH):
+                tokens = slice(c * CH, (c + 1) * CH)
+                for t in range(PACK):
+                    cols = slice(t * P, (t + 1) * P)
+                    mm(hbank[c][:, t, :], w2q[z][:, cols], w2s[z][:, cols], xq[z][:, tokens], xs[z][:, tokens],
+                       z == 0 and t == 0, z == PASSES - 1 and t == PACK - 1)
 
         first = load_x(0, 0)
         nc.sync.dma_start(offsets[:], offs)
-        gather(0, 0, first)
-        for j in range(1, 4):
-            plane(0, j)
-            load_scales(j - 1)
-        quant_x(0)
-        plane(1, 0)
-        load_scales(3)
-        for j in range(1, 3):
-            plane(1, j)
+        gather_x(0, 0, first)
+        for j in range(1, PACK):
+            gather_x(0, j, load_x(0, j))
+            load_w1_scales(j - 1)
+        quantise_x(0)
+
+        gather_x(1, 0, load_x(1, 0))
+        load_w1_scales(PACK - 1)
+        for j in range(1, PACK - 1):
+            gather_x(1, j, load_x(1, j))
+
         raw0 = load_w2(0, 0, H)
         deal_w2(nc.scalar.copy, 0, raw0, 0, P, 0, 1)
         deal_w2(nc.vector.tensor_copy, 0, raw0, 0, P, 1, PACK)
-        nc.vector.quantize_mx(w2q[0][:].bitcast(FP8X4), w2s[0][:], w2g[0][:].rearrange("p t m j -> p (t m j)"))
-        for c in range(NCH):
-            for t in range(PACK):
-                h_pass(0, c, t)
-        plane(1, 3)
-        quant_x(1)
+        quantise_w2(0, 0, PACK)
+        h_pass(0)
+
+        gather_x(1, PACK - 1, load_x(1, PACK - 1))
+        quantise_x(1)
+
         raw1a = load_w2(1, 0, H // 2)
         raw1b = load_w2(1, H // 2, H)
-        w1q = keep.tile([P, 2, N], U32, name="w1q", align_bytes=64)
+        w1q = keep.tile([P, PASSES, N], U32, name="w1q", align_bytes=64)
         nc.sync.dma_start(w1q[:].bitcast(I32), w1_words.rearrange("z p n t -> p z (n t)").bitcast(I32))
         w3q = keep.tile([P, N], U32, name="w3q", align_bytes=64)
         nc.sync.dma_start(w3q[:].bitcast(I32), w3_words[0].rearrange("p n t -> p (n t)").bitcast(I32))
+        for r in range(PACK):
+            load_w3_scales(r)
+
         deal_w2(nc.scalar.copy, 1, raw1a, 0, P // 2, 0, PACK)
-        deal_w2(nc.scalar.copy, 1, raw1b, P // 2, P, 3, PACK)
-        deal_w2(nc.vector.tensor_copy, 1, raw1b, P // 2, P, 0, 3)
+        deal_w2(nc.scalar.copy, 1, raw1b, P // 2, P, PACK - 1, PACK)
+        deal_w2(nc.vector.tensor_copy, 1, raw1b, P // 2, P, 0, PACK - 1)
         for t in range(0, PACK, 2):
-            ws = slice(t * P, (t + 2) * P)
-            nc.vector.quantize_mx(w2q[1][:, ws].bitcast(FP8X4), w2s[1][:, ws], w2g[1][:, t:t + 2, :, :].rearrange("p t m j -> p (t m j)"))
+            quantise_w2(1, t, t + 2)
+        h_pass(1)
+
         for c in range(NCH):
-            for t in range(PACK):
-                h_pass(1, c, t)
+            tokens = slice(c * CH, (c + 1) * CH)
+            for z in range(PASSES):
+                mm(obank[c][:], w1q[:, z, :], s1[:, z, :], xq[z][:, tokens], xs[z][:, tokens], z == 0, False)
+
+        res = keep.tile([P, S], F32, name="res")
         for c in range(NCH):
-            w1_pass(0, c)
-            w1_pass(1, c)
-        for c in range(NCH):
-            copy = nc.scalar.copy if c % 2 == 1 else nc.vector.tensor_copy
+            copy = nc.vector.tensor_copy if c % 2 == 0 else nc.scalar.copy
             hg = keep.tile([P, CH, PACK], BF16, name=f"hg{c}", align_bytes=64)
             copy(hg[:], hbank[c][:].rearrange("p t n -> p n t"))
             hq = keep.tile([P, CH], U32, name=f"hq{c}", align_bytes=64)
             hs = keep.tile([P, CH], U8, name=f"hs{c}", align_bytes=64)
             nc.vector.quantize_mx(hq[:].bitcast(FP8X4), hs[:], hg[:].rearrange("p n t -> p (n t)"))
             mm(obank[c][:], w3q[:], s3[:], hq[:], hs[:], False, True)
-            res = keep.tile([P, CH], F32, name=f"res{c}")
-            nc.scalar.copy(res[:], obank[c][:])
-            nc.sync.dma_start(out[:, c * CH:(c + 1) * CH], res[:])
+
+        for c in range(NCH):
+            copy = nc.scalar.copy if c % 2 == 0 else nc.vector.tensor_copy
+            copy(res[:, c * CH:(c + 1) * CH], obank[c][:])
+            if c % 2 == 1:
+                pair = slice((c - 1) * CH, (c + 1) * CH)
+                nc.sync.dma_start(out[:, pair], res[:, pair])

from contextlib import ExitStack

import concourse.mybir as mybir

K, T, S, H, N = 1024, 2048, 512, 512, 128
FLOPS = 2 * S * (K * H + K * N + H * N)

F32 = mybir.dt.float32
BF16 = mybir.dt.bfloat16
I32 = mybir.dt.int32
U32 = mybir.dt.uint32
U16 = mybir.dt.uint16
U8 = mybir.dt.uint8
FP8X4 = mybir.dt.float8_e4m3fn_x4

P = 128
PACK = 4
KP = P * PACK
PASSES = K // KP
QUADRANT = 32
BLOCKS = KP // 32
CH = 128
NCH = S // CH


def tile_picked_lora_none_e_kernel(tc, xT, w1_words, w1_scales, w2, w3_words, w3_scales, offs, out):
    nc = tc.nc
    with ExitStack() as ctx:
        keep = ctx.enter_context(tc.tile_pool(name="keep", bufs=1))
        psum = ctx.enter_context(tc.psum_pool(name="psum", bufs=1))

        offsets = keep.tile([P, S // 16], U16, name="offsets")

        s1 = keep.tile([P, PASSES, N], U8, name="s1", align_bytes=64)
        s3 = keep.tile([P, N], U8, name="s3", align_bytes=64)
        nc.vector.memset(s1[:], 0)
        nc.vector.memset(s3[:], 0)

        w2g = [keep.tile([P, PACK, P, PACK], BF16, name=f"w2g{z}", align_bytes=64) for z in range(PASSES)]
        w2q = [keep.tile([P, H], U32, name=f"w2q{z}", align_bytes=64) for z in range(PASSES)]
        w2s = [keep.tile([P, H], U8, name=f"w2s{z}", align_bytes=64) for z in range(PASSES)]
        xg = [keep.tile([P, S, PACK], BF16, name=f"xg{z}", align_bytes=64) for z in range(PASSES)]
        xq = [keep.tile([P, S], U32, name=f"xq{z}", align_bytes=64) for z in range(PASSES)]
        xs = [keep.tile([P, S], U8, name=f"xs{z}", align_bytes=64) for z in range(PASSES)]

        hbank = [psum.tile([P, PACK, CH], F32, name=f"hbank{c}") for c in range(NCH)]
        obank = [psum.tile([P, CH], F32, name=f"obank{c}") for c in range(NCH)]

        def load_w2(z, col0, col1):
            raw = keep.tile([P, PACK, col1 - col0], F32, name=f"w2raw{z}_{col0}")
            nc.sync.dma_start(raw[:], w2[z * KP:(z + 1) * KP, col0:col1].rearrange("(p j) c -> p j c", j=PACK))
            return raw

        def deal_w2(copy, z, raw, m0, m1, t0, t1):
            src = raw[:].rearrange("p j (m t) -> p m t j", t=PACK)[:, :, t0:t1, :]
            copy(w2g[z][:, t0:t1, m0:m1, :].rearrange("p t m j -> p m t j"), src)

        def quantise_w2(z, t0, t1):
            cols = slice(t0 * P, t1 * P)
            values = w2g[z][:, t0:t1, :, :].rearrange("p t m j -> p (t m j)")
            nc.vector.quantize_mx(w2q[z][:, cols].bitcast(FP8X4), w2s[z][:, cols], values)

        def load_x(z, j):
            win = keep.tile([P, T], F32, name=f"x{z}_{j}")
            nc.sync.dma_start(win[:], xT[z * KP + j:(z + 1) * KP:PACK, :])
            return win

        def gather_x(z, j, win):
            nc.vector.tensor_copy(xg[z][:, :, j], win[:].indirect(offsets[:]))

        def quantise_x(z):
            nc.vector.quantize_mx(xq[z][:].bitcast(FP8X4), xs[z][:], xg[z][:].rearrange("p s j -> p (s j)"))

        def load_w1_scales(r):
            rows = w1_scales[:, r:BLOCKS:PACK, :].rearrange("z q c -> q z c")
            nc.sync.dma_start(s1[r:P:QUADRANT, :, :].bitcast(I32), rows.bitcast(I32))

        def load_w3_scales(r):
            nc.sync.dma_start(s3[r:P:QUADRANT, :].bitcast(I32), w3_scales[0, r:BLOCKS:PACK, :].bitcast(I32))

        def mm(dst, lhs_words, lhs_scales, rhs_words, rhs_scales, start, stop):
            nc.tensor.matmul_mx(dst, lhs_words.bitcast(FP8X4), lhs_scales, rhs_words.bitcast(FP8X4), rhs_scales,
                                start=start, stop=stop)

        def h_pass(z):
            for c in range(NCH):
                tokens = slice(c * CH, (c + 1) * CH)
                for t in range(PACK):
                    cols = slice(t * P, (t + 1) * P)
                    mm(hbank[c][:, t, :], w2q[z][:, cols], w2s[z][:, cols], xq[z][:, tokens], xs[z][:, tokens],
                       z == 0 and t == 0, z == PASSES - 1 and t == PACK - 1)

        first = load_x(0, 0)
        nc.sync.dma_start(offsets[:], offs)
        gather_x(0, 0, first)
        for j in range(1, PACK):
            gather_x(0, j, load_x(0, j))
            load_w1_scales(j - 1)
        quantise_x(0)

        gather_x(1, 0, load_x(1, 0))
        load_w1_scales(PACK - 1)
        for j in range(1, PACK - 1):
            gather_x(1, j, load_x(1, j))

        raw0 = load_w2(0, 0, H)
        deal_w2(nc.scalar.copy, 0, raw0, 0, P, 0, 1)
        deal_w2(nc.vector.tensor_copy, 0, raw0, 0, P, 1, PACK)
        quantise_w2(0, 0, PACK)
        h_pass(0)

        gather_x(1, PACK - 1, load_x(1, PACK - 1))
        quantise_x(1)

        raw1a = load_w2(1, 0, H // 2)
        raw1b = load_w2(1, H // 2, H)
        w1q = keep.tile([P, PASSES, N], U32, name="w1q", align_bytes=64)
        nc.sync.dma_start(w1q[:].bitcast(I32), w1_words.rearrange("z p n t -> p z (n t)").bitcast(I32))
        w3q = keep.tile([P, N], U32, name="w3q", align_bytes=64)
        nc.sync.dma_start(w3q[:].bitcast(I32), w3_words[0].rearrange("p n t -> p (n t)").bitcast(I32))
        for r in range(PACK):
            load_w3_scales(r)

        deal_w2(nc.scalar.copy, 1, raw1a, 0, P // 2, 0, PACK)
        deal_w2(nc.scalar.copy, 1, raw1b, P // 2, P, PACK - 1, PACK)
        deal_w2(nc.vector.tensor_copy, 1, raw1b, P // 2, P, 0, PACK - 1)
        for t in range(0, PACK, 2):
            quantise_w2(1, t, t + 2)
        h_pass(1)

        for c in range(NCH):
            tokens = slice(c * CH, (c + 1) * CH)
            for z in range(PASSES):
                mm(obank[c][:], w1q[:, z, :], s1[:, z, :], xq[z][:, tokens], xs[z][:, tokens], z == 0, False)

        res = keep.tile([P, S], F32, name="res")
        for c in range(NCH):
            copy = nc.vector.tensor_copy if c % 2 == 0 else nc.scalar.copy
            hg = keep.tile([P, CH, PACK], BF16, name=f"hg{c}", align_bytes=64)
            copy(hg[:], hbank[c][:].rearrange("p t n -> p n t"))
            hq = keep.tile([P, CH], U32, name=f"hq{c}", align_bytes=64)
            hs = keep.tile([P, CH], U8, name=f"hs{c}", align_bytes=64)
            nc.vector.quantize_mx(hq[:].bitcast(FP8X4), hs[:], hg[:].rearrange("p n t -> p (n t)"))
            mm(obank[c][:], w3q[:], s3[:], hq[:], hs[:], False, True)

        for c in range(NCH):
            copy = nc.scalar.copy if c % 2 == 0 else nc.vector.tensor_copy
            copy(res[:, c * CH:(c + 1) * CH], obank[c][:])
            if c % 2 == 1:
                pair = slice((c - 1) * CH, (c + 1) * CH)
                nc.sync.dma_start(out[:, pair], res[:, pair])
